import numpy as np
import ml_dtypes


def mxq(x, axis, fmt="e4m3"):
    dtype, down = {"e4m3": (ml_dtypes.float8_e4m3fn, 7), "e5m2": (ml_dtypes.float8_e5m2, 14)}[fmt]
    v = np.moveaxis(np.asarray(x, np.float32).astype(ml_dtypes.bfloat16).astype(np.float64), axis, -1)
    blocks = v.reshape(v.shape[:-1] + (-1, 32))
    amax = np.abs(blocks).max(-1, keepdims=True)
    byte = np.maximum(np.where(amax > 0, np.frexp(amax)[1] - 1 + 127, 0) - down, 1)
    scale = np.exp2(byte - 127.0)
    codes = (blocks / scale).astype(np.float32).astype(dtype).astype(np.float64)
    return np.moveaxis((codes * scale).reshape(v.shape), -1, axis)


WIDE = False


def mx_kscale(k):
    if not WIDE:
        return np.ones(k)
    levels = np.array([10, -10, 5, -5, 0])
    if k % 512:
        return np.exp2(np.random.permutation(np.resize(levels, k // 32))).repeat(32)
    a = np.empty((k // 512, 16))
    for p in range(k // 512):
        a[p, :8] = np.random.permutation(np.resize(levels, 8))
        for g in range(8):
            far = levels[np.abs(levels - a[p, g]) >= 10]
            a[p, g + 8] = far[np.random.randint(len(far))]
    return np.exp2(a.ravel()).repeat(32)


def f64(x):
    return np.asarray(x).astype(np.float64)


def striped(idx):
    return np.tile(idx.reshape(-1, 16).T, (8, 1)).astype(np.uint16)


def unstriped(offs):
    return offs[:16].T.reshape(-1).astype(np.int64)


def pack_weight(w):
    k, n = w.shape
    w = f64(np.asarray(w, np.float32).astype(ml_dtypes.bfloat16)).reshape(k // 32, 32, n)
    amax = np.abs(w).max(1)
    byte = np.clip(np.where(amax > 0, np.frexp(amax)[1] - 1 + 127 - 7, 1), 1, 254)
    scaled = (w * np.exp2(127.0 - byte)[:, None, :]).reshape(k, n).astype(np.float32)
    words = np.ascontiguousarray(scaled.reshape(k // 512, 128, 4, n).transpose(0, 1, 3, 2)).astype(ml_dtypes.float8_e4m3fn).view(np.uint8)
    return words, np.ascontiguousarray(byte.astype(np.uint8).reshape(k // 512, 16, n))


def unpack_weight(words, scales):
    g, p, n, _ = words.shape
    vals = np.ascontiguousarray(words).view(ml_dtypes.float8_e4m3fn).astype(np.float64) * np.repeat(np.exp2(scales.astype(np.float64) - 127.0), 8, axis=1)[..., None]
    return vals.transpose(0, 1, 3, 2).reshape(g * 512, n)


def relu(v):
    return np.maximum(v, 0.0)


K, T, S, H, N = 1024, 4096, 1024, 512, 256
P = 2 ** 7


def setup_inputs():
    n = np.random.standard_normal
    s = mx_kscale(K)[:, None]
    u = mx_kscale(H)
    packed_xT = pack_weight(n((K, T)) * s)
    return {
        "x_words": packed_xT[0],
        "x_scales": packed_xT[1],
        "w1": (n((K, H)) / np.sqrt(K) / s * u).astype(np.float32),
        "w2": (n((H, N)) / np.sqrt(H) / u[:, None]).astype(np.float32),
        "noise": (0.3 * n((H, S)) * u[:, None]).astype(np.float32),
        "obs": (-n((N, 1))).astype(np.float32),
        "prior": (np.tile(np.random.uniform(0.5, 1.5, S), (P, 1))).astype(np.float32),
        "offs": striped(np.random.randint(0, T, S)),
    }


def reference(x_words, x_scales, w1, w2, noise, obs, prior, offs):
    xq = unpack_weight(x_words, x_scales)[:, unstriped(offs)]
    h = relu((mxq(f64(w1), 0, "e4m3").T @ xq) + f64(noise))
    dd = (mxq(f64(w2), 0, "e4m3").T @ mxq(h, 0, "e4m3")) + f64(obs)
    return f64(prior)[:1] / ((dd) ** 2 + 1.0)

@@ -1,0 +1,241 @@
+from contextlib import ExitStack
+
+import concourse.mybir as mybir
+from concourse.masks import make_identity
+
+K, T, S, H, N = 1024, 4096, 1024, 512, 256
+FLOPS = 2 * S * H * (K + N)
+BYTES = K * T + K * T // 32 + 4 * (K * H + H * N + H * S + N + S + N * S) + 2 * 128 * (S // 16)
+
+F32 = mybir.dt.float32
+BF16 = mybir.dt.bfloat16
+I32 = mybir.dt.int32
+U32 = mybir.dt.uint32
+U16 = mybir.dt.uint16
+U8 = mybir.dt.uint8
+FP8X4 = mybir.dt.float8_e4m3fn_x4
+ACT = mybir.ActivationFunctionType
+ALU = mybir.AluOpType
+
+P = 128
+PACK = 4
+K_PASS = P * PACK
+PASSES = K // K_PASS
+HALF = S // 2
+CHUNK = 128
+NOISE_LOADS = ((0, 128), (128, 128), (256, 256), (512, 256), (768, 256))
+GROUPS = ((0, 128), (128, 128), (256, 256), (512, 256), (768, 128), (896, 128))
+W1_LOADS = ((0, 0, 512), (1, 0, 256), (1, 256, 256))
+WARM_PASSES = 4
+M_TILES = N // P
+
+
+def tile_picked_ypart_cauchy_p_kernel(tc, x_words, x_scales, w1, w2, noise, obs, prior, offs, out):
+    nc = tc.nc
+    with ExitStack() as ctx:
+        keep = ctx.enter_context(tc.tile_pool(name="keep", bufs=1))
+        ps_h = ctx.enter_context(tc.psum_pool(name="ps_h", bufs=6))
+        ps_d = ctx.enter_context(tc.psum_pool(name="ps_d", bufs=2))
+
+        def sb(name, shape, dtype):
+            return keep.tile(shape, dtype, name=name, align_bytes=64)
+
+        offsets = keep.tile([P, S // 16], U16, name="offsets")
+        w1_raw = [sb("w1_raw%d" % i, [P, PACK, w], F32) for i, (o, c0, w) in enumerate(W1_LOADS)]
+        word_table = [sb("word_table%d" % o, [P, T], U32) for o in range(PASSES)]
+        scale_table = sb("scale_table", [P, T], U8)
+        w2_raw = sb("w2_raw", [P, PACK, N], F32)
+        noise_sb = [sb("noise%d" % q, [P, PACK, w], F32) for q, (j0, w) in enumerate(NOISE_LOADS)]
+        prior_cols = sb("prior_cols", [P, S // P], F32)
+        obs_sb = sb("obs_sb", [P, M_TILES], F32)
+
+        def load_w1(i):
+            o, c0, w = W1_LOADS[i]
+            rows = w1[o * K_PASS : (o + 1) * K_PASS, c0 : c0 + w]
+            nc.sync.dma_start(out=w1_raw[i][:], in_=rows.rearrange("(p j) c -> p j c", j=PACK))
+
+        def load_words(o):
+            nc.sync.dma_start(out=word_table[o][:].bitcast(I32), in_=x_words[o].rearrange("p n t -> p (n t)").bitcast(I32))
+
+        def load_scales(o):
+            for quad in range(4):
+                row = 32 * quad + 4 * o
+                nc.sync.dma_start(
+                    out=scale_table[row : row + 4, :].bitcast(I32),
+                    in_=x_scales[o, 4 * quad : 4 * quad + 4, :].bitcast(I32),
+                )
+
+        def load_noise(q):
+            j0, w = NOISE_LOADS[q]
+            cols = noise[:, j0 : j0 + w]
+            nc.sync.dma_start(out=noise_sb[q][:], in_=cols.rearrange("(p t) n -> p t n", t=PACK))
+
+        nc.vector.memset(scale_table[:].bitcast(I32), 0)
+        nc.sync.dma_start(offsets[:], offs)
+        load_w1(0)
+        load_scales(0)
+        load_words(0)
+        nc.sync.dma_start(out=prior_cols[:], in_=prior[0:1, :].rearrange("o (n e) -> (o n) e", e=S // P))
+        load_scales(1)
+        load_words(1)
+        nc.sync.dma_start(out=obs_sb[:], in_=obs.rearrange("(p t) o -> p (t o)", t=M_TILES))
+        load_w1(1)
+        load_w1(2)
+        nc.sync.dma_start(out=w2_raw[:], in_=w2.rearrange("(p j) c -> p j c", j=PACK))
+        for q in range(len(NOISE_LOADS)):
+            load_noise(q)
+
+        one = sb("one", [P, 1], F32)
+        nc.vector.memset(one[:], 1.0)
+        warm = sb("warm", [P, 1], F32)
+        nc.scalar.activation(out=warm[:], in_=one[:], func=ACT.Abs_reciprocal_sqrt, bias=one[:])
+
+        def deal(copy, dealt, raw):
+            copy(
+                out=dealt.rearrange("p t m j -> p m j t"),
+                in_=raw.rearrange("p j (m t) -> p m j t", t=dealt.shape[1]),
+            )
+
+        def quantize(codes, scales, values):
+            nc.vector.quantize_mx(out=codes.bitcast(FP8X4), scales=scales, in_=values)
+
+        w1_codes = [sb("w1_codes%d" % o, [P, H], U32) for o in range(PASSES)]
+        w1_scales = [sb("w1_scales%d" % o, [P, H], U8) for o in range(PASSES)]
+
+        w1_dealt = [sb("w1_dealt%d" % o, [P, PACK, P, PACK], BF16) for o in range(PASSES)]
+
+        def deal_w1(copy, i):
+            o, c0, w = W1_LOADS[i]
+            deal(copy, w1_dealt[o][:, :, c0 // PACK : (c0 + w) // PACK, :], w1_raw[i][:])
+
+        def quantize_w1(o):
+            for t in range(PACK):
+                cols = slice(t * P, (t + 1) * P)
+                quantize(w1_codes[o][:, cols], w1_scales[o][:, cols], w1_dealt[o][:, t].rearrange("p m j -> p (m j)"))
+
+        picked_scales = sb("picked_scales", [P, S], U8)
+        picked_words = [[sb("picked_words%d_%d" % (o, h), [P, HALF], U32) for h in range(2)] for o in range(PASSES)]
+
+        def gather_words(o):
+            for h in range(2):
+                part = offsets[:, h * HALF // 16 : (h + 1) * HALF // 16]
+                nc.vector.tensor_copy(picked_words[o][h][:], word_table[o][:].indirect(part))
+
+        deal_w1(nc.scalar.copy, 0)
+        quantize_w1(0)
+
+        identity = sb("identity", [P, P], F32)
+        make_identity(nc, identity[:])
+        prior_rows = sb("prior_rows", [P, S], F32)
+        for b in range(2):
+            spread = ps_d.tile([P, 4, P], F32, name="spread", tag="dd")
+            for e in range(4):
+                column = prior_cols[:, 4 * b + e : 4 * b + e + 1]
+                nc.tensor.transpose(spread[:, e, :], column.to_broadcast([P, P]), identity[:])
+            nc.scalar.copy(
+                out=prior_rows[:].rearrange("p (n e) -> p n e", e=S // P)[:, :, 4 * b : 4 * b + 4],
+                in_=spread[:].rearrange("p e n -> p n e"),
+            )
+
+        gather_words(0)
+        nc.vector.tensor_copy(picked_scales[:], scale_table[:].indirect(offsets[:]))
+        gather_words(1)
+        idle = ps_d.tile([P, HALF], F32, name="idle", tag="dd")
+        for i in range(WARM_PASSES):
+            nc.tensor.matmul_mx(
+                out=idle[:],
+                lhsT=w1_codes[0][:, 0:P].bitcast(FP8X4),
+                lhsT_scale=w1_scales[0][:, 0:P],
+                rhs=picked_words[1][0][:].bitcast(FP8X4),
+                rhs_scale=picked_scales[4:P, 0:HALF],
+                start=True,
+                stop=True,
+            )
+        deal_w1(nc.scalar.copy, 1)
+        deal_w1(nc.vector.tensor_copy, 2)
+        quantize_w1(1)
+
+        w2_codes = sb("w2_codes", [P, N], U32)
+        w2_scales = sb("w2_scales", [P, N], U8)
+        w2_dealt = sb("w2_dealt", [P, M_TILES, P, PACK], BF16)
+        deal(nc.scalar.copy, w2_dealt[:], w2_raw[:])
+
+        summed = [sb("summed%d" % g, [P, w, PACK], BF16) for g, (j0, w) in enumerate(GROUPS)]
+        hidden = [sb("hidden%d" % g, [P, w * PACK], BF16) for g, (j0, w) in enumerate(GROUPS)]
+        weights = [sb("weights%d" % g, [P, M_TILES, w], F32) for g, (j0, w) in enumerate(GROUPS)]
+
+        def first_layer(j0):
+            g = max(i for i in range(len(GROUPS)) if GROUPS[i][0] <= j0)
+            bank = ps_h.tile([P, PACK, CHUNK], F32, name="bank")
+            half, at = divmod(j0, HALF)
+            for t in range(PACK):
+                cols = slice(t * P, (t + 1) * P)
+                for o in range(PASSES):
+                    nc.tensor.matmul_mx(
+                        out=bank[:, t, :],
+                        lhsT=w1_codes[o][:, cols].bitcast(FP8X4),
+                        lhsT_scale=w1_scales[o][:, cols],
+                        rhs=picked_words[o][half][:, at : at + CHUNK].bitcast(FP8X4),
+                        rhs_scale=picked_scales[4 * o : P, j0 : j0 + CHUNK],
+                        start=(o == 0),
+                        stop=(o == PASSES - 1),
+                    )
+            q = max(i for i in range(len(NOISE_LOADS)) if NOISE_LOADS[i][0] <= j0)
+            nat = j0 - NOISE_LOADS[q][0]
+            gat = j0 - GROUPS[g][0]
+            nc.vector.tensor_tensor(
+                out=summed[g][:, gat : gat + CHUNK, :].rearrange("p (c i) t -> p c t i", i=2),
+                in0=bank[:].rearrange("p t (c i) -> p c t i", i=2),
+                in1=noise_sb[q][:, :, nat : nat + CHUNK].rearrange("p t (c i) -> p c t i", i=2),
+                op=ALU.add,
+            )
+
+        def rectify(g):
+            nc.vector.tensor_scalar_max(hidden[g][:], summed[g][:].rearrange("p n t -> p (n t)"), 0.0)
+
+        def second_layer(g):
+            w = GROUPS[g][1]
+            h_codes = sb("h_codes%d" % g, [P, w], U32)
+            h_scales = sb("h_scales%d" % g, [P, w], U8)
+            quantize(h_codes[:], h_scales[:], hidden[g][:])
+            dd = ps_d.tile([P, M_TILES, w], F32, name="dd", tag="dd")
+            squares = sb("squares%d" % g, [P, M_TILES, w], F32)
+            roots = sb("roots%d" % g, [P, M_TILES, w], F32)
+            for t in range(M_TILES):
+                cols = slice(t * P, (t + 1) * P)
+                nc.tensor.matmul_mx(
+                    out=dd[:, t, :],
+                    lhsT=w2_codes[:, cols].bitcast(FP8X4),
+                    lhsT_scale=w2_scales[:, cols],
+                    rhs=h_codes[:].bitcast(FP8X4),
+                    rhs_scale=h_scales[:],
+                    start=True,
+                    stop=True,
+                )
+            for t in range(M_TILES):
+                nc.scalar.activation(out=squares[:, t, :], in_=dd[:, t, :], func=ACT.Square, bias=obs_sb[:, t : t + 1])
+            nc.scalar.activation(out=roots[:], in_=squares[:], func=ACT.Abs_reciprocal_sqrt, bias=one[:])
+            nc.scalar.activation(out=weights[g][:], in_=roots[:], func=ACT.Square)
+
+        def weigh_and_store(g):
+            j0, w = GROUPS[g]
+            result = sb("result%d" % g, [P, M_TILES, w], F32)
+            nc.vector.tensor_tensor(
+                out=result[:],
+                in0=weights[g][:],
+                in1=prior_rows[:, j0 : j0 + w].unsqueeze(1).to_broadcast([P, M_TILES, w]),
+                op=ALU.mult,
+            )
+            nc.sync.dma_start(out=out[:, j0 : j0 + w].rearrange("(p t) n -> p t n", t=M_TILES), in_=result[:])
+
+        chunks = S // CHUNK
+        last_chunk = [(j0 + w) // CHUNK - 1 for j0, w in GROUPS]
+        for step in range(chunks + 4):
+            if step < chunks:
+                first_layer(step * CHUNK)
+            if step == 1:
+                quantize(w2_codes[:], w2_scales[:], w2_dealt[:].rearrange("p t m j -> p (t m j)"))
+            for lag, stage in ((1, rectify), (2, second_layer), (4, weigh_and_store)):
+                for g in range(len(GROUPS)):
+                    if last_chunk[g] + lag == step:
+                        stage(g)

@@ -25,8 +25,8 @@ HALF = S // 2
 CHUNK = 128
 NOISE_LOADS = ((0, 128), (128, 128), (256, 256), (512, 256), (768, 256))
 GROUPS = ((0, 128), (128, 128), (256, 256), (512, 256), (768, 128), (896, 128))
-W1_LOADS = ((0, 0, 512), (1, 0, 256), (1, 256, 256))
-WARM_PASSES = 4
+STORES = ((0, 256), (256, 256), (512, 256), (768, 128), (896, 128))
+W1_LOADS = ((0, 0, 512), (1, 0, 512))
 M_TILES = N // P
 
 
@@ -34,8 +34,8 @@ def tile_picked_ypart_cauchy_p_kernel(tc, x_words, x_scales, w1, w2, noise, obs,
     nc = tc.nc
     with ExitStack() as ctx:
         keep = ctx.enter_context(tc.tile_pool(name="keep", bufs=1))
-        ps_h = ctx.enter_context(tc.psum_pool(name="ps_h", bufs=6))
-        ps_d = ctx.enter_context(tc.psum_pool(name="ps_d", bufs=2))
+        ps_h = ctx.enter_context(tc.psum_pool(name="ps_h", bufs=3))
+        ps_d = ctx.enter_context(tc.psum_pool(name="ps_d", bufs=3))
 
         def sb(name, shape, dtype):
             return keep.tile(shape, dtype, name=name, align_bytes=64)
@@ -54,8 +54,9 @@ def tile_picked_ypart_cauchy_p_kernel(tc, x_words, x_scales, w1, w2, noise, obs,
             rows = w1[o * K_PASS : (o + 1) * K_PASS, c0 : c0 + w]
             nc.sync.dma_start(out=w1_raw[i][:], in_=rows.rearrange("(p j) c -> p j c", j=PACK))
 
-        def load_words(o):
-            nc.sync.dma_start(out=word_table[o][:].bitcast(I32), in_=x_words[o].rearrange("p n t -> p (n t)").bitcast(I32))
+        def load_words(o, c0, c1):
+            words = x_words[o].rearrange("p n t -> p (n t)").bitcast(I32)
+            nc.sync.dma_start(out=word_table[o][:, c0:c1].bitcast(I32), in_=words[:, c0:c1])
 
         def load_scales(o):
             for quad in range(4):
@@ -74,13 +75,12 @@ def tile_picked_ypart_cauchy_p_kernel(tc, x_words, x_scales, w1, w2, noise, obs,
         nc.sync.dma_start(offsets[:], offs)
         load_w1(0)
         load_scales(0)
-        load_words(0)
+        load_words(0, 0, T)
         nc.sync.dma_start(out=prior_cols[:], in_=prior[0:1, :].rearrange("o (n e) -> (o n) e", e=S // P))
         load_scales(1)
-        load_words(1)
-        nc.sync.dma_start(out=obs_sb[:], in_=obs.rearrange("(p t) o -> p (t o)", t=M_TILES))
         load_w1(1)
-        load_w1(2)
+        nc.sync.dma_start(out=obs_sb[:], in_=obs.rearrange("(p t) o -> p (t o)", t=M_TILES))
+        load_words(1, 0, T)
         nc.sync.dma_start(out=w2_raw[:], in_=w2.rearrange("(p j) c -> p j c", j=PACK))
         for q in range(len(NOISE_LOADS)):
             load_noise(q)
@@ -139,21 +139,9 @@ def tile_picked_ypart_cauchy_p_kernel(tc, x_words, x_scales, w1, w2, noise, obs,
 
         gather_words(0)
         nc.vector.tensor_copy(picked_scales[:], scale_table[:].indirect(offsets[:]))
-        gather_words(1)
-        idle = ps_d.tile([P, HALF], F32, name="idle", tag="dd")
-        for i in range(WARM_PASSES):
-            nc.tensor.matmul_mx(
-                out=idle[:],
-                lhsT=w1_codes[0][:, 0:P].bitcast(FP8X4),
-                lhsT_scale=w1_scales[0][:, 0:P],
-                rhs=picked_words[1][0][:].bitcast(FP8X4),
-                rhs_scale=picked_scales[4:P, 0:HALF],
-                start=True,
-                stop=True,
-            )
         deal_w1(nc.scalar.copy, 1)
-        deal_w1(nc.vector.tensor_copy, 2)
         quantize_w1(1)
+        gather_words(1)
 
         w2_codes = sb("w2_codes", [P, N], U32)
         w2_scales = sb("w2_scales", [P, N], U8)
@@ -163,6 +151,9 @@ def tile_picked_ypart_cauchy_p_kernel(tc, x_words, x_scales, w1, w2, noise, obs,
         summed = [sb("summed%d" % g, [P, w, PACK], BF16) for g, (j0, w) in enumerate(GROUPS)]
         hidden = [sb("hidden%d" % g, [P, w * PACK], BF16) for g, (j0, w) in enumerate(GROUPS)]
         weights = [sb("weights%d" % g, [P, M_TILES, w], F32) for g, (j0, w) in enumerate(GROUPS)]
+
+        squares = [sb("squares%d" % g, [P, M_TILES, w], F32) for g, (j0, w) in enumerate(GROUPS)]
+        roots = [sb("roots%d" % g, [P, M_TILES, w], F32) for g, (j0, w) in enumerate(GROUPS)]
 
         def first_layer(j0):
             g = max(i for i in range(len(GROUPS)) if GROUPS[i][0] <= j0)
@@ -197,10 +188,10 @@ def tile_picked_ypart_cauchy_p_kernel(tc, x_words, x_scales, w1, w2, noise, obs,
             w = GROUPS[g][1]
             h_codes = sb("h_codes%d" % g, [P, w], U32)
             h_scales = sb("h_scales%d" % g, [P, w], U8)
+            if g == 0:
+                quantize(w2_codes[:], w2_scales[:], w2_dealt[:].rearrange("p t m j -> p (t m j)"))
             quantize(h_codes[:], h_scales[:], hidden[g][:])
             dd = ps_d.tile([P, M_TILES, w], F32, name="dd", tag="dd")
-            squares = sb("squares%d" % g, [P, M_TILES, w], F32)
-            roots = sb("roots%d" % g, [P, M_TILES, w], F32)
             for t in range(M_TILES):
                 cols = slice(t * P, (t + 1) * P)
                 nc.tensor.matmul_mx(
@@ -213,29 +204,44 @@ def tile_picked_ypart_cauchy_p_kernel(tc, x_words, x_scales, w1, w2, noise, obs,
                     stop=True,
                 )
             for t in range(M_TILES):
-                nc.scalar.activation(out=squares[:, t, :], in_=dd[:, t, :], func=ACT.Square, bias=obs_sb[:, t : t + 1])
-            nc.scalar.activation(out=roots[:], in_=squares[:], func=ACT.Abs_reciprocal_sqrt, bias=one[:])
-            nc.scalar.activation(out=weights[g][:], in_=roots[:], func=ACT.Square)
+                nc.scalar.activation(out=squares[g][:, t, :], in_=dd[:, t, :], func=ACT.Square, bias=obs_sb[:, t : t + 1])
+
+        def root(g):
+            nc.scalar.activation(out=roots[g][:], in_=squares[g][:], func=ACT.Abs_reciprocal_sqrt, bias=one[:])
+
+        def square_root_again(g):
+            nc.scalar.activation(out=weights[g][:], in_=roots[g][:], func=ACT.Square)
+
+        results = [sb("result%d" % i, [P, M_TILES, w], F32) for i, (j0, w) in enumerate(STORES)]
 
         def weigh_and_store(g):
             j0, w = GROUPS[g]
-            result = sb("result%d" % g, [P, M_TILES, w], F32)
+            i = max(i for i in range(len(STORES)) if STORES[i][0] <= j0)
+            s0, sw = STORES[i]
             nc.vector.tensor_tensor(
-                out=result[:],
+                out=results[i][:, :, j0 - s0 : j0 - s0 + w],
                 in0=weights[g][:],
                 in1=prior_rows[:, j0 : j0 + w].unsqueeze(1).to_broadcast([P, M_TILES, w]),
                 op=ALU.mult,
             )
-            nc.sync.dma_start(out=out[:, j0 : j0 + w].rearrange("(p t) n -> p t n", t=M_TILES), in_=result[:])
+            if j0 + w == s0 + sw:
+                nc.sync.dma_start(out=out[:, s0 : s0 + sw].rearrange("(p t) n -> p t n", t=M_TILES), in_=results[i][:])
 
         chunks = S // CHUNK
         last_chunk = [(j0 + w) // CHUNK - 1 for j0, w in GROUPS]
-        for step in range(chunks + 4):
+        for step in range(chunks + 1):
             if step < chunks:
                 first_layer(step * CHUNK)
-            if step == 1:
-                quantize(w2_codes[:], w2_scales[:], w2_dealt[:].rearrange("p t m j -> p (t m j)"))
-            for lag, stage in ((1, rectify), (2, second_layer), (4, weigh_and_store)):
-                for g in range(len(GROUPS)):
-                    if last_chunk[g] + lag == step:
-                        stage(g)
+            if step - 1 in last_chunk:
+                g = last_chunk.index(step - 1)
+                rectify(g)
+                if g >= 2:
+                    weigh_and_store(g - 2)
+                second_layer(g)
+                if g >= 1:
+                    square_root_again(g - 1)
+                root(g)
+        last = len(GROUPS) - 1
+        square_root_again(last)
+        weigh_and_store(last - 1)
+        weigh_and_store(last)

@@ -49,22 +49,14 @@ def tile_picked_ypart_cauchy_p_kernel(tc, x_words, x_scales, w1, w2, noise, obs,
         prior_cols = sb("prior_cols", [P, S // P], F32)
         obs_sb = sb("obs_sb", [P, M_TILES], F32)
 
-        def load_w1(i):
+        def load_w1(i, j0, j1):
             o, c0, w = W1_LOADS[i]
             rows = w1[o * K_PASS : (o + 1) * K_PASS, c0 : c0 + w]
-            nc.sync.dma_start(out=w1_raw[i][:], in_=rows.rearrange("(p j) c -> p j c", j=PACK))
+            nc.sync.dma_start(out=w1_raw[i][:, j0:j1, :], in_=rows.rearrange("(p j) c -> p j c", j=PACK)[:, j0:j1, :])
 
         def load_words(o, c0, c1):
             words = x_words[o].rearrange("p n t -> p (n t)").bitcast(I32)
             nc.sync.dma_start(out=word_table[o][:, c0:c1].bitcast(I32), in_=words[:, c0:c1])
-
-        def load_scales(o):
-            for quad in range(4):
-                row = 32 * quad + 4 * o
-                nc.sync.dma_start(
-                    out=scale_table[row : row + 4, :].bitcast(I32),
-                    in_=x_scales[o, 4 * quad : 4 * quad + 4, :].bitcast(I32),
-                )
 
         def load_noise(q):
             j0, w = NOISE_LOADS[q]
@@ -73,14 +65,16 @@ def tile_picked_ypart_cauchy_p_kernel(tc, x_words, x_scales, w1, w2, noise, obs,
 
         nc.vector.memset(scale_table[:].bitcast(I32), 0)
         nc.sync.dma_start(offsets[:], offs)
-        load_w1(0)
-        load_scales(0)
+        load_w1(0, 0, 2)
+        nc.sync.dma_start(
+            out=scale_table[0:P:4, :].bitcast(I32), in_=x_scales.rearrange("o q n -> (o q) n").bitcast(I32)
+        )
+        load_w1(0, 2, 4)
         load_words(0, 0, T)
         nc.sync.dma_start(out=prior_cols[:], in_=prior[0:1, :].rearrange("o (n e) -> (o n) e", e=S // P))
-        load_scales(1)
-        load_w1(1)
-        nc.sync.dma_start(out=obs_sb[:], in_=obs.rearrange("(p t) o -> p (t o)", t=M_TILES))
+        load_w1(1, 0, 4)
         load_words(1, 0, T)
+        nc.sync.dma_start(out=obs_sb[:], in_=obs.rearrange("(p t) o -> p (t o)", t=M_TILES))
         nc.sync.dma_start(out=w2_raw[:], in_=w2.rearrange("(p j) c -> p j c", j=PACK))
         for q in range(len(NOISE_LOADS)):
             load_noise(q)
@@ -121,6 +115,16 @@ def tile_picked_ypart_cauchy_p_kernel(tc, x_words, x_scales, w1, w2, noise, obs,
                 part = offsets[:, h * HALF // 16 : (h + 1) * HALF // 16]
                 nc.vector.tensor_copy(picked_words[o][h][:], word_table[o][:].indirect(part))
 
+        picked_rows = sb("picked_rows", [P, S], U8)
+        nc.vector.tensor_copy(picked_rows[:], scale_table[:].indirect(offsets[:]))
+        nc.vector.memset(picked_scales[:].bitcast(I32), 0)
+        for o in range(PASSES):
+            for r in range(4):
+                first = 4 * (16 * o + r)
+                nc.gpsimd.dma_start(
+                    out=picked_scales[4 * o + r : P : 32, :].bitcast(I32),
+                    in_=picked_rows[first : first + 49 : 16, :].bitcast(I32),
+                )
         deal_w1(nc.scalar.copy, 0)
         quantize_w1(0)
 
@@ -138,7 +142,6 @@ def tile_picked_ypart_cauchy_p_kernel(tc, x_words, x_scales, w1, w2, noise, obs,
             )
 
         gather_words(0)
-        nc.vector.tensor_copy(picked_scales[:], scale_table[:].indirect(offsets[:]))
         deal_w1(nc.scalar.copy, 1)
         quantize_w1(1)
         gather_words(1)

from contextlib import ExitStack

import concourse.mybir as mybir
from concourse.masks import make_identity

K, T, S, H, N = 1024, 4096, 1024, 512, 256
FLOPS = 2 * S * H * (K + N)
BYTES = K * T + K * T // 32 + 4 * (K * H + H * N + H * S + N + S + N * S) + 2 * 128 * (S // 16)

F32 = mybir.dt.float32
BF16 = mybir.dt.bfloat16
I32 = mybir.dt.int32
U32 = mybir.dt.uint32
U16 = mybir.dt.uint16
U8 = mybir.dt.uint8
FP8X4 = mybir.dt.float8_e4m3fn_x4
ACT = mybir.ActivationFunctionType
ALU = mybir.AluOpType

P = 128
PACK = 4
K_PASS = P * PACK
PASSES = K // K_PASS
HALF = S // 2
CHUNK = 128
NOISE_LOADS = ((0, 128), (128, 128), (256, 256), (512, 256), (768, 256))
GROUPS = ((0, 128), (128, 128), (256, 256), (512, 256), (768, 128), (896, 128))
STORES = ((0, 256), (256, 256), (512, 256), (768, 128), (896, 128))
W1_LOADS = ((0, 0, 512), (1, 0, 512))
M_TILES = N // P


def tile_picked_ypart_cauchy_p_kernel(tc, x_words, x_scales, w1, w2, noise, obs, prior, offs, out):
    nc = tc.nc
    with ExitStack() as ctx:
        keep = ctx.enter_context(tc.tile_pool(name="keep", bufs=1))
        ps_h = ctx.enter_context(tc.psum_pool(name="ps_h", bufs=3))
        ps_d = ctx.enter_context(tc.psum_pool(name="ps_d", bufs=3))

        def sb(name, shape, dtype):
            return keep.tile(shape, dtype, name=name, align_bytes=64)

        offsets = keep.tile([P, S // 16], U16, name="offsets")
        w1_raw = [sb("w1_raw%d" % i, [P, PACK, w], F32) for i, (o, c0, w) in enumerate(W1_LOADS)]
        word_table = [sb("word_table%d" % o, [P, T], U32) for o in range(PASSES)]
        scale_table = sb("scale_table", [P, T], U8)
        w2_raw = sb("w2_raw", [P, PACK, N], F32)
        noise_sb = [sb("noise%d" % q, [P, PACK, w], F32) for q, (j0, w) in enumerate(NOISE_LOADS)]
        prior_cols = sb("prior_cols", [P, S // P], F32)
        obs_sb = sb("obs_sb", [P, M_TILES], F32)

        def load_w1(i, j0, j1):
            o, c0, w = W1_LOADS[i]
            rows = w1[o * K_PASS : (o + 1) * K_PASS, c0 : c0 + w]
            nc.sync.dma_start(out=w1_raw[i][:, j0:j1, :], in_=rows.rearrange("(p j) c -> p j c", j=PACK)[:, j0:j1, :])

        def load_words(o, c0, c1):
            words = x_words[o].rearrange("p n t -> p (n t)").bitcast(I32)
            nc.sync.dma_start(out=word_table[o][:, c0:c1].bitcast(I32), in_=words[:, c0:c1])

        def load_noise(q):
            j0, w = NOISE_LOADS[q]
            cols = noise[:, j0 : j0 + w]
            nc.sync.dma_start(out=noise_sb[q][:], in_=cols.rearrange("(p t) n -> p t n", t=PACK))

        nc.vector.memset(scale_table[:].bitcast(I32), 0)
        nc.sync.dma_start(offsets[:], offs)
        load_w1(0, 0, 2)
        nc.sync.dma_start(
            out=scale_table[0:P:4, :].bitcast(I32), in_=x_scales.rearrange("o q n -> (o q) n").bitcast(I32)
        )
        load_w1(0, 2, 4)
        load_words(0, 0, T)
        nc.sync.dma_start(out=prior_cols[:], in_=prior[0:1, :].rearrange("o (n e) -> (o n) e", e=S // P))
        load_w1(1, 0, 4)
        load_words(1, 0, T)
        nc.sync.dma_start(out=obs_sb[:], in_=obs.rearrange("(p t) o -> p (t o)", t=M_TILES))
        nc.sync.dma_start(out=w2_raw[:], in_=w2.rearrange("(p j) c -> p j c", j=PACK))
        for q in range(len(NOISE_LOADS)):
            load_noise(q)

        one = sb("one", [P, 1], F32)
        nc.vector.memset(one[:], 1.0)
        warm = sb("warm", [P, 1], F32)
        nc.scalar.activation(out=warm[:], in_=one[:], func=ACT.Abs_reciprocal_sqrt, bias=one[:])

        def deal(copy, dealt, raw):
            copy(
                out=dealt.rearrange("p t m j -> p m j t"),
                in_=raw.rearrange("p j (m t) -> p m j t", t=dealt.shape[1]),
            )

        def quantize(codes, scales, values):
            nc.vector.quantize_mx(out=codes.bitcast(FP8X4), scales=scales, in_=values)

        w1_codes = [sb("w1_codes%d" % o, [P, H], U32) for o in range(PASSES)]
        w1_scales = [sb("w1_scales%d" % o, [P, H], U8) for o in range(PASSES)]

        w1_dealt = [sb("w1_dealt%d" % o, [P, PACK, P, PACK], BF16) for o in range(PASSES)]

        def deal_w1(copy, i):
            o, c0, w = W1_LOADS[i]
            deal(copy, w1_dealt[o][:, :, c0 // PACK : (c0 + w) // PACK, :], w1_raw[i][:])

        def quantize_w1(o):
            for t in range(PACK):
                cols = slice(t * P, (t + 1) * P)
                quantize(w1_codes[o][:, cols], w1_scales[o][:, cols], w1_dealt[o][:, t].rearrange("p m j -> p (m j)"))

        picked_scales = sb("picked_scales", [P, S], U8)
        picked_words = [[sb("picked_words%d_%d" % (o, h), [P, HALF], U32) for h in range(2)] for o in range(PASSES)]

        def gather_words(o):
            for h in range(2):
                part = offsets[:, h * HALF // 16 : (h + 1) * HALF // 16]
                nc.vector.tensor_copy(picked_words[o][h][:], word_table[o][:].indirect(part))

        picked_rows = sb("picked_rows", [P, S], U8)
        nc.vector.tensor_copy(picked_rows[:], scale_table[:].indirect(offsets[:]))
        nc.vector.memset(picked_scales[:].bitcast(I32), 0)
        for o in range(PASSES):
            for r in range(4):
                first = 4 * (16 * o + r)
                nc.gpsimd.dma_start(
                    out=picked_scales[4 * o + r : P : 32, :].bitcast(I32),
                    in_=picked_rows[first : first + 49 : 16, :].bitcast(I32),
                )
        deal_w1(nc.scalar.copy, 0)
        quantize_w1(0)

        identity = sb("identity", [P, P], F32)
        make_identity(nc, identity[:])
        prior_rows = sb("prior_rows", [P, S], F32)
        for b in range(2):
            spread = ps_d.tile([P, 4, P], F32, name="spread", tag="dd")
            for e in range(4):
                column = prior_cols[:, 4 * b + e : 4 * b + e + 1]
                nc.tensor.transpose(spread[:, e, :], column.to_broadcast([P, P]), identity[:])
            nc.scalar.copy(
                out=prior_rows[:].rearrange("p (n e) -> p n e", e=S // P)[:, :, 4 * b : 4 * b + 4],
                in_=spread[:].rearrange("p e n -> p n e"),
            )

        gather_words(0)
        deal_w1(nc.scalar.copy, 1)
        quantize_w1(1)
        gather_words(1)

        w2_codes = sb("w2_codes", [P, N], U32)
        w2_scales = sb("w2_scales", [P, N], U8)
        w2_dealt = sb("w2_dealt", [P, M_TILES, P, PACK], BF16)
        deal(nc.scalar.copy, w2_dealt[:], w2_raw[:])

        summed = [sb("summed%d" % g, [P, w, PACK], BF16) for g, (j0, w) in enumerate(GROUPS)]
        hidden = [sb("hidden%d" % g, [P, w * PACK], BF16) for g, (j0, w) in enumerate(GROUPS)]
        weights = [sb("weights%d" % g, [P, M_TILES, w], F32) for g, (j0, w) in enumerate(GROUPS)]

        squares = [sb("squares%d" % g, [P, M_TILES, w], F32) for g, (j0, w) in enumerate(GROUPS)]
        roots = [sb("roots%d" % g, [P, M_TILES, w], F32) for g, (j0, w) in enumerate(GROUPS)]

        def first_layer(j0):
            g = max(i for i in range(len(GROUPS)) if GROUPS[i][0] <= j0)
            bank = ps_h.tile([P, PACK, CHUNK], F32, name="bank")
            half, at = divmod(j0, HALF)
            for t in range(PACK):
                cols = slice(t * P, (t + 1) * P)
                for o in range(PASSES):
                    nc.tensor.matmul_mx(
                        out=bank[:, t, :],
                        lhsT=w1_codes[o][:, cols].bitcast(FP8X4),
                        lhsT_scale=w1_scales[o][:, cols],
                        rhs=picked_words[o][half][:, at : at + CHUNK].bitcast(FP8X4),
                        rhs_scale=picked_scales[4 * o : P, j0 : j0 + CHUNK],
                        start=(o == 0),
                        stop=(o == PASSES - 1),
                    )
            q = max(i for i in range(len(NOISE_LOADS)) if NOISE_LOADS[i][0] <= j0)
            nat = j0 - NOISE_LOADS[q][0]
            gat = j0 - GROUPS[g][0]
            nc.vector.tensor_tensor(
                out=summed[g][:, gat : gat + CHUNK, :].rearrange("p (c i) t -> p c t i", i=2),
                in0=bank[:].rearrange("p t (c i) -> p c t i", i=2),
                in1=noise_sb[q][:, :, nat : nat + CHUNK].rearrange("p t (c i) -> p c t i", i=2),
                op=ALU.add,
            )

        def rectify(g):
            nc.vector.tensor_scalar_max(hidden[g][:], summed[g][:].rearrange("p n t -> p (n t)"), 0.0)

        def second_layer(g):
            w = GROUPS[g][1]
            h_codes = sb("h_codes%d" % g, [P, w], U32)
            h_scales = sb("h_scales%d" % g, [P, w], U8)
            if g == 0:
                quantize(w2_codes[:], w2_scales[:], w2_dealt[:].rearrange("p t m j -> p (t m j)"))
            quantize(h_codes[:], h_scales[:], hidden[g][:])
            dd = ps_d.tile([P, M_TILES, w], F32, name="dd", tag="dd")
            for t in range(M_TILES):
                cols = slice(t * P, (t + 1) * P)
                nc.tensor.matmul_mx(
                    out=dd[:, t, :],
                    lhsT=w2_codes[:, cols].bitcast(FP8X4),
                    lhsT_scale=w2_scales[:, cols],
                    rhs=h_codes[:].bitcast(FP8X4),
                    rhs_scale=h_scales[:],
                    start=True,
                    stop=True,
                )
            for t in range(M_TILES):
                nc.scalar.activation(out=squares[g][:, t, :], in_=dd[:, t, :], func=ACT.Square, bias=obs_sb[:, t : t + 1])

        def root(g):
            nc.scalar.activation(out=roots[g][:], in_=squares[g][:], func=ACT.Abs_reciprocal_sqrt, bias=one[:])

        def square_root_again(g):
            nc.scalar.activation(out=weights[g][:], in_=roots[g][:], func=ACT.Square)

        results = [sb("result%d" % i, [P, M_TILES, w], F32) for i, (j0, w) in enumerate(STORES)]

        def weigh_and_store(g):
            j0, w = GROUPS[g]
            i = max(i for i in range(len(STORES)) if STORES[i][0] <= j0)
            s0, sw = STORES[i]
            nc.vector.tensor_tensor(
                out=results[i][:, :, j0 - s0 : j0 - s0 + w],
                in0=weights[g][:],
                in1=prior_rows[:, j0 : j0 + w].unsqueeze(1).to_broadcast([P, M_TILES, w]),
                op=ALU.mult,
            )
            if j0 + w == s0 + sw:
                nc.sync.dma_start(out=out[:, s0 : s0 + sw].rearrange("(p t) n -> p t n", t=M_TILES), in_=results[i][:])

        chunks = S // CHUNK
        last_chunk = [(j0 + w) // CHUNK - 1 for j0, w in GROUPS]
        for step in range(chunks + 1):
            if step < chunks:
                first_layer(step * CHUNK)
            if step - 1 in last_chunk:
                g = last_chunk.index(step - 1)
                rectify(g)
                if g >= 2:
                    weigh_and_store(g - 2)
                second_layer(g)
                if g >= 1:
                    square_root_again(g - 1)
                root(g)
        last = len(GROUPS) - 1
        square_root_again(last)
        weigh_and_store(last - 1)
        weigh_and_store(last)
